import numpy as np, ml_dtypes
CORES = [78,86,94,102,110,118]
N = 6
import mx_ref
NC, NB = 256, 3
A = np.float32(0.0125)
SRC = [[(r - i) % N for i in range(NB)] for r in range(N)]
BF = ml_dtypes.bfloat16
def cut(t, i, w=512):
    return t[:, w * i:w * i + w]
def tile(rs):
    return np.stack(rs, axis=2).reshape(128, -1).astype(BF)
def setup_inputs(rng):
    def f(*shape):
        return mx_ref.flush((rng.standard_normal(shape, dtype=np.float32) * np.exp2(rng.integers(-2, 3, shape[:-1] + (1,)))).astype(BF))
    return {"q": f(N, 128, 4 * NC), "k": f(N, 128, 4 * 512), "v": f(N, 128, 512)}
def setup_inputs_blocks(rng):
    d = setup_inputs(rng)
    for k in ("v",): d[k] = mx_ref.spread(d[k], rng, 4)
    for k in ("q", "k"): d[k] = mx_ref.spread(d[k], rng, 1)
    return d
def setup_inputs_wide(rng):
    d = setup_inputs(rng)
    for k in ("v",): d[k] = mx_ref.flush((d[k].astype(np.float32) * np.exp2(rng.integers(-8, 9, (N, 1, 1))).astype(np.float32)).astype(BF))
    return d
def setup_inputs_sharp(rng):
    d = setup_inputs(rng); v = d["q"].astype(np.float32).reshape(N, 128, -1, 4)
    d["q"] = mx_ref.flush((v * np.exp2(rng.integers(-2, 4, (N, 1, v.shape[2], 1))).astype(np.float32)).reshape(d["q"].shape).astype(BF))
    return d
def setup_inputs_offset(rng):
    d = setup_inputs(rng); v = d["k"].astype(np.float32).reshape(N, 128, -1, 4)
    d["k"] = mx_ref.flush((v + 12 * rng.standard_normal((1, 128, 1, 4), dtype=np.float32)).reshape(d["k"].shape).astype(BF))
    return d
def reference(q, k, v, own=None):
    ONE = mx_ref.quantize(np.ones((128, 512), BF))
    K = [[mx_ref.quantize(cut(k[j], b)) for b in range(4)] for j in range(N)]; V = [mx_ref.quantize(v[j]) for j in range(N)]
    lo = np.zeros((N, NB, NC), np.float32); hi = lo.copy(); c = lo.copy(); w = lo.copy(); wlo = lo.copy(); whi = lo.copy(); p = np.zeros((N, NB, 128, 4 * NC), BF); o = np.zeros((N, 128, NC), np.float32)
    for r in range(N):
        Q = mx_ref.quantize(q[r])
        S = [[mx_ref.matmul(K[j][b], Q) * A for b in range(4)] for j in SRC[r]]
        lo[r] = [np.max(s, axis=(0, 1)) for s in S]; hi[r] = lo[r].max(axis=0) + 8
        c[r] = lo[r] if own is None else own["c"][r]
        for i in range(NB):
            p[r][i] = tile([np.exp(np.maximum(s - c[r][i], -20).astype(np.float64)).astype(np.float32) for s in S[i]])
        use = p[r] if own is None else own["p"][r]
        e = np.exp((c[r] - c[r].max(axis=0)).astype(np.float64)); wlo[r] = e * (1 - 4e-5); whi[r] = e * (1 + 4e-5)
        w[r] = e if own is None else own["w"][r]
        num = den = 0
        for i in range(NB):
            P = mx_ref.quantize(use[i])
            num = num + w[r][i].astype(np.float64) * mx_ref.matmul(V[SRC[r][i]], P); den = den + w[r][i].astype(np.float64) * mx_ref.matmul(ONE, P)
        o[r] = (num / den).astype(np.float32)
    return {"c": c, "c__lo": lo, "c__hi": hi, "p": p, "w": w, "w__lo": wlo, "w__hi": whi, "o": o}

@@ -1,0 +1,227 @@
+import math
+from concourse.mybir import dt, AluOpType, AxisListType, ActivationFunctionType
+
+F32, BF, CODE, U8 = "float32", "bfloat16", "float8_e4m3fn_x4", "uint8"
+SCRATCH = {
+    "kin": ("sbuf", [128, 2048], BF), "vin": ("sbuf", [128, 512], BF), "qin": ("sbuf", [128, 1024], BF),
+    "one": ("sbuf", [128, 512], BF),
+    "qc": ("sbuf", [128, 256], CODE), "qs": ("sbuf", [128, 256], U8),
+    "onec": ("sbuf", [128, 128], CODE), "ones": ("sbuf", [128, 128], U8),
+    "fw": ("sbuf", [128, 512], F32), "gw": ("sbuf", [128, 512], F32), "wbc": ("sbuf", [128, 512], F32),
+    "fr": ("sbuf", [128, 256], F32), "gr": ("sbuf", [128, 256], F32), "rbc": ("sbuf", [128, 256], F32),
+    "craw": ("sbuf", [128, 8], F32), "dcol": ("sbuf", [128, 4], F32), "lcol": ("sbuf", [128, 4], F32),
+    "t4": ("sbuf", [128, 4], F32), "t01": ("sbuf", [128, 2], F32), "den": ("sbuf", [128, 2], F32),
+    "onef": ("sbuf", [128, 256], F32), "n1": ("sbuf", [128, 256], F32), "n2": ("sbuf", [128, 256], F32),
+    "ob": ("sbuf", [128, 256], F32),
+    "ps": ("psum", [128, 4096], F32),
+}
+for _i in range(3):
+    SCRATCH["kvc%d" % _i] = ("sbuf", [128, 640], CODE)
+    SCRATCH["kvs%d" % _i] = ("sbuf", [128, 640], U8)
+    SCRATCH["ssc%d" % _i] = ("sbuf", [128, 1024], F32)
+    SCRATCH["pt%d" % _i] = ("sbuf", [128, 1024], BF)
+    SCRATCH["pc%d" % _i] = ("sbuf", [128, 256], CODE)
+    SCRATCH["pp%d" % _i] = ("sbuf", [128, 256], U8)
+    SCRATCH["fc%d" % _i] = ("sbuf", [128, 256], F32)
+    SCRATCH["gc%d" % _i] = ("sbuf", [128, 256], F32)
+    SCRATCH["cbc%d" % _i] = ("sbuf", [128, 256], F32)
+
+SEMAPHORES = ["dve", "act", "pe", "pool", "sent", "arr1", "arr2", "ld_k0", "ld_k1", "ld_v", "ld_q", "stored"]
+
+SCALE = 0.0125
+FLOOR = math.exp(-20.0)
+
+
+def rank_program(g, core, T, topo):
+    rank = T.rank_of(core)
+    if rank is None:
+        return
+    n_ranks = len(T.cores)
+    ALU, ACT = AluOpType, ActivationFunctionType
+    queue = {"dve": g.vector, "act": g.scalar, "pe": g.tensor, "pool": g, "sync": g.sync}
+    count = {}
+    seen = {}
+    writer = {}
+    readers = {}
+
+    def need(q, ticket):
+        if ticket is None:
+            return
+        s, n = ticket
+        if seen.get((q, s), 0) < n:
+            queue[q].wait_ge(T.sem[s], n)
+            seen[(q, s)] = n
+
+    def deps(q, reads, writes):
+        for k in reads:
+            need(q, writer.get(k))
+        for k in writes:
+            need(q, writer.get(k))
+            for t in readers.get(k, []):
+                need(q, t)
+
+    def note(ticket, reads, writes):
+        for k in reads:
+            readers.setdefault(k, []).append(ticket)
+        for k in writes:
+            writer[k] = ticket
+            readers[k] = []
+
+    def op(q, reads, writes, make):
+        deps(q, reads, writes)
+        count[q] = count.get(q, 0) + 1
+        make().then_inc(T.sem[q], 1)
+        note((q, count[q]), reads, writes)
+
+    def dma(q, sem, out, in_, reads, writes):
+        deps(q, reads, writes)
+        count[sem] = count.get(sem, 0) + 16
+        queue[q].dma_start(out, in_).then_inc(T.sem[sem], 16)
+        note((sem, count[sem]), reads, writes)
+
+    def bank(j, n):
+        return T.ps[:, 512 * j:512 * j + n]
+
+    V, S, P = g.vector, g.scalar, g.tensor
+
+    dma("sync", "ld_k0", T.kin[:, 0:1024], T.k[:, 0:1024], [], ["kin0"])
+    dma("act", "ld_k1", T.kin[:, 1024:2048], T.k[:, 1024:2048], [], ["kin1"])
+    dma("sync", "ld_v", T.vin[:], T.v[:], [], ["vin"])
+    dma("act", "ld_q", T.qin[:], T.q[:], [], ["qin"])
+
+    op("dve", [], ["one"], lambda: V.memset(T.one[:], 1.0))
+    op("dve", ["one"], ["ONE"], lambda: V.quantize_mx(T.onec[:], T.ones[:], T.one[:]))
+    op("dve", [], ["fc0"], lambda: V.memset(T.fc0[0:32, :], 0.0))
+
+    op("dve", ["kin0"], ["kv0"], lambda: V.quantize_mx(T.kvc0[:, 0:256], T.kvs0[:, 0:256], T.kin[:, 0:1024]))
+    op("dve", ["kin1"], ["kv0"], lambda: V.quantize_mx(T.kvc0[:, 256:512], T.kvs0[:, 256:512], T.kin[:, 1024:2048]))
+    op("dve", ["vin"], ["kv0"], lambda: V.quantize_mx(T.kvc0[:, 512:640], T.kvs0[:, 512:640], T.vin[:]))
+    op("dve", ["qin"], ["Q"], lambda: V.quantize_mx(T.qc[:], T.qs[:], T.qin[:]))
+
+    deps("pool", ["kv0"], [])
+    for d in (2, 1):
+        dst = T.cores[(rank + d) % n_ranks]
+        rid, pid, _ = topo.addr(dst)
+        mask = topo.mask(core, dst)
+        eng = bin(mask).count("1")
+        g.remote_dma(out_ap=T["kvc%d" % d][:].bitcast(dt.uint8), in_ap=T.kvc0[:].bitcast(dt.uint8),
+                     remote_sem=T.sem["arr%d" % d], local_sem=T.sem.sent, pid=pid, routing_id=rid, dma_engine_mask=mask)
+        g.remote_dma(out_ap=T["kvs%d" % d][:], in_ap=T.kvs0[:],
+                     remote_sem=T.sem["arr%d" % d], local_sem=T.sem.sent, pid=pid, routing_id=rid, dma_engine_mask=mask)
+        count["sent"] = count.get("sent", 0) + 2 * eng
+        src = T.cores[(rank - d) % n_ranks]
+        count["arr%d" % d] = 2 * bin(topo.mask(src, core)).count("1")
+        writer["kv%d" % d] = ("arr%d" % d, count["arr%d" % d])
+
+    def to_row(f, gt, fkey, gkey, width):
+        for a in (1, 2, 3):
+            op("dve", [fkey], [fkey], lambda: V.tensor_copy(f[0:32, 32 * a:width:128], f[32 * a:32 * a + 32, 0:width:128]))
+        op("dve", [fkey], [gkey], lambda: V.transpose(gt[0:32, 0:width], f[0:32, 0:width]))
+
+    def scores(i, prev):
+        kc, ks, kv = T["kvc%d" % i], T["kvs%d" % i], "kv%d" % i
+        fc, gc, cbc, ssc = T["fc%d" % i], T["gc%d" % i], T["cbc%d" % i], T["ssc%d" % i]
+        for h in (0, 1):
+            op("pe", [kv, "Q"], ["bank%d" % (2 + h)], lambda: P.matmul_mx(
+                bank(2 + h, 512), T.qc[:, 128 * h:128 * h + 128], T.qs[:, 128 * h:128 * h + 128],
+                kc[:, 0:512], ks[:, 0:512], True, True))
+        for h in (0, 1):
+            raw = T.craw[:, 2 * i + h:2 * i + h + 1]
+            op("dve", [], ["bank%d" % (2 + h), "craw%d" % i], lambda: V.tensor_reduce(
+                raw, bank(2 + h, 512), AxisListType.X, ALU.max))
+            col = fc[:, 128 * h:128 * h + 1]
+            if prev is None:
+                op("dve", ["craw%d" % i], ["fc%d" % i], lambda: V.tensor_scalar(col, raw, SCALE, None, ALU.mult))
+            else:
+                op("dve", ["craw%d" % i, "fc%d" % prev], ["fc%d" % i], lambda: V.tensor_scalar(
+                    col, raw, SCALE, T["fc%d" % prev][:, 128 * h:128 * h + 1], ALU.mult, ALU.max))
+        for pair in (0, 2):
+            for b in (pair, pair + 1):
+                op("pe", [kv, "Q"], ["bank%d" % (b % 2)], lambda: P.matmul_mx(
+                    bank(b % 2, 256), kc[:, 128 * b:128 * b + 128], ks[:, 128 * b:128 * b + 128],
+                    T.qc[:], T.qs[:], True, True))
+            for b in (pair, pair + 1):
+                op("act", [], ["bank%d" % (b % 2), "ssc%d.%d" % (i, b)], lambda: S.activation(
+                    ssc[:, 256 * b:256 * b + 256], bank(b % 2, 256), ACT.Copy, scale=SCALE))
+        to_row(fc, gc, "fc%d" % i, "gc%d" % i, 256)
+        op("pool", ["gc%d" % i], ["cbc%d" % i], lambda: g.partition_broadcast(cbc[:], gc[0:1, :], 128))
+        dma("sync", "stored", T.c[i:i + 1, :], gc[0:1, :], ["gc%d" % i], [])
+
+    def probs(i):
+        cbc, ssc, pt = T["cbc%d" % i], T["ssc%d" % i], T["pt%d" % i]
+        for b in range(4):
+            x = ssc[:, 256 * b:256 * b + 256]
+            op("dve", ["cbc%d" % i], ["ssc%d.%d" % (i, b)], lambda: V.tensor_tensor(x, x, cbc[:], ALU.subtract))
+            op("act", ["ssc%d.%d" % (i, b)], ["pt%d.%d" % (i, b)], lambda: S.activation(pt[:, b:1024:4], x, ACT.Exp))
+        for b in range(4):
+            y = pt[:, b:1024:4]
+            op("dve", [], ["pt%d.%d" % (i, b)], lambda: V.tensor_scalar(y, y, FLOOR, None, ALU.max))
+        tiles = ["pt%d.%d" % (i, b) for b in range(4)]
+        op("dve", tiles, ["P%d" % i], lambda: V.quantize_mx(T["pc%d" % i][:], T["pp%d" % i][:], pt[:]))
+        dma("sync", "stored", T.p[i], pt[:], tiles, [])
+
+    def sums(i):
+        pc, pp = T["pc%d" % i], T["pp%d" % i]
+        for h in (0, 1):
+            op("pe", ["P%d" % i, "ONE"], ["bank%d" % (4 + h)], lambda: P.matmul_mx(
+                bank(4 + h, 128), pc[:, 128 * h:128 * h + 128], pp[:, 128 * h:128 * h + 128],
+                T.onec[:], T.ones[:], True, True))
+
+    def values(i, j):
+        op("pe", ["P%d" % i, "kv%d" % i], ["bank%d" % j], lambda: P.matmul_mx(
+            bank(j, 256), T["kvc%d" % i][:, 512:640], T["kvs%d" % i][:, 512:640],
+            T["pc%d" % i][:], T["pp%d" % i][:], True, True))
+
+    def keep_sums(slot):
+        for h in (0, 1):
+            op("dve", [], ["bank%d" % (4 + h), "lcol"], lambda: V.tensor_copy(
+                T.lcol[:, 2 * slot + h:2 * slot + h + 1], bank(4 + h, 1)))
+
+    x, y, z = 0, 2, 1
+
+    scores(x, None)
+    for name in ("fc1", "fc2", "fw", "fr"):
+        op("dve", [], [name], lambda: V.memset(T[name][0:32, :], 0.0))
+    op("dve", [], ["onef"], lambda: V.memset(T.onef[0:1, :], 1.0))
+    probs(x)
+    sums(x)
+    values(x, 6)
+    keep_sums(0)
+
+    scores(y, x)
+    probs(y)
+    sums(y)
+    values(y, 7)
+    keep_sums(1)
+
+    scores(z, y)
+    for slot, i in ((0, x), (1, y)):
+        op("dve", ["fc%d" % i, "fc%d" % z], ["dcol"], lambda: V.tensor_tensor(
+            T.dcol[:, 2 * slot:2 * slot + 2], T["fc%d" % i][:, 0:256:128], T["fc%d" % z][:, 0:256:128], ALU.subtract))
+    op("act", ["dcol"], ["fw"], lambda: S.activation(T.fw[:, 0:512:128], T.dcol[:, 0:4], ACT.Exp))
+    op("dve", ["fw", "lcol"], ["t4"], lambda: V.tensor_tensor(T.t4[:], T.lcol[:], T.fw[:, 0:512:128], ALU.mult))
+    to_row(T.fw, T.gw, "fw", "gw", 512)
+    op("pool", ["gw"], ["wbc"], lambda: g.partition_broadcast(T.wbc[:], T.gw[0:1, :], 128))
+    op("dve", ["t4"], ["t01"], lambda: V.tensor_tensor(T.t01[:], T.t4[:, 0:2], T.t4[:, 2:4], ALU.add))
+    dma("sync", "stored", T.w[x:x + 1, :], T.gw[0:1, 0:256], ["gw"], [])
+    dma("sync", "stored", T.w[y:y + 1, :], T.gw[0:1, 256:512], ["gw"], [])
+    dma("sync", "stored", T.w[z:z + 1, :], T.onef[0:1, :], ["onef"], [])
+    probs(z)
+    sums(z)
+    values(z, 0)
+
+    op("dve", ["wbc"], ["bank6", "n1"], lambda: V.tensor_tensor(T.n1[:], bank(6, 256), T.wbc[:, 0:256], ALU.mult))
+    for h in (0, 1):
+        op("dve", ["t01"], ["bank%d" % (4 + h), "den"], lambda: V.tensor_tensor(
+            T.den[:, h:h + 1], bank(4 + h, 1), T.t01[:, h:h + 1], ALU.add))
+    op("dve", ["den"], ["fr"], lambda: V.reciprocal(T.fr[:, 0:256:128], T.den[:]))
+    to_row(T.fr, T.gr, "fr", "gr", 256)
+    op("pool", ["gr"], ["rbc"], lambda: g.partition_broadcast(T.rbc[:], T.gr[0:1, :], 128))
+    op("dve", ["wbc"], ["bank7", "n2"], lambda: V.tensor_tensor(T.n2[:], bank(7, 256), T.wbc[:, 256:512], ALU.mult))
+    op("dve", ["n2"], ["n1"], lambda: V.tensor_tensor(T.n1[:], T.n1[:], T.n2[:], ALU.add))
+    op("dve", [], ["bank0", "n1"], lambda: V.tensor_tensor(T.n1[:], bank(0, 256), T.n1[:], ALU.add))
+    op("dve", ["n1", "rbc"], ["ob"], lambda: V.tensor_tensor(T.ob[:], T.n1[:], T.rbc[:], ALU.mult))
+    dma("sync", "stored", T.o[:], T.ob[:], ["ob"], [])
+
+    for s in SEMAPHORES:
+        need("pool", (s, count[s]))

@@ -7,12 +7,11 @@ SCRATCH = {
     "one": ("sbuf", [128, 512], BF),
     "qc": ("sbuf", [128, 256], CODE), "qs": ("sbuf", [128, 256], U8),
     "onec": ("sbuf", [128, 128], CODE), "ones": ("sbuf", [128, 128], U8),
-    "fw": ("sbuf", [128, 512], F32), "gw": ("sbuf", [128, 512], F32), "wbc": ("sbuf", [128, 512], F32),
+    "fw": ("sbuf", [128, 256], F32), "gw": ("sbuf", [128, 256], F32), "wbc": ("sbuf", [128, 256], F32),
     "fr": ("sbuf", [128, 256], F32), "gr": ("sbuf", [128, 256], F32), "rbc": ("sbuf", [128, 256], F32),
-    "craw": ("sbuf", [128, 8], F32), "dcol": ("sbuf", [128, 4], F32), "lcol": ("sbuf", [128, 4], F32),
-    "t4": ("sbuf", [128, 4], F32), "t01": ("sbuf", [128, 2], F32), "den": ("sbuf", [128, 2], F32),
-    "onef": ("sbuf", [128, 256], F32), "n1": ("sbuf", [128, 256], F32), "n2": ("sbuf", [128, 256], F32),
-    "ob": ("sbuf", [128, 256], F32),
+    "craw": ("sbuf", [128, 8], F32), "dcol": ("sbuf", [128, 2], F32), "lcol": ("sbuf", [128, 2], F32),
+    "t01": ("sbuf", [128, 2], F32), "den": ("sbuf", [128, 2], F32),
+    "onef": ("sbuf", [128, 256], F32), "n1": ("sbuf", [128, 256], F32), "ob": ("sbuf", [128, 256], F32),
     "ps": ("psum", [128, 4096], F32),
 }
 for _i in range(3):
@@ -26,15 +25,46 @@ for _i in range(3):
     SCRATCH["gc%d" % _i] = ("sbuf", [128, 256], F32)
     SCRATCH["cbc%d" % _i] = ("sbuf", [128, 256], F32)
 
-SEMAPHORES = ["dve", "act", "pe", "pool", "sent", "arr1", "arr2", "ld_k0", "ld_k1", "ld_v", "ld_q", "stored"]
+SEMAPHORES = ["dve", "act", "pe", "pool", "sent", "arr1", "arr2", "ld_k0", "ld_k1", "ld_v", "ld_q", "stored", "hc", "hs"]
 
 SCALE = 0.0125
 FLOOR = math.exp(-20.0)
 
 
+def engines(mask):
+    return bin(mask).count("1")
+
+
+def helper_of(c, T, topo):
+    far = T.cores[(T.rank_of(c) + 2) % len(T.cores)]
+    for h in range(topo.CHIPS * topo.CORES_PER_CHIP):
+        if h != c and topo.chip(h) == topo.chip(c) and topo.die(h) != topo.die(c) \
+                and T.rank_of(h) is None and topo.may_write(h, far):
+            return h
+    return None
+
+
+def forward(g, core, owner, T, topo):
+    far = T.cores[(T.rank_of(owner) + 2) % len(T.cores)]
+    near = T.cores[(T.rank_of(owner) + 1) % len(T.cores)]
+    got = engines(topo.mask(owner, core) & ~topo.mask(owner, near))
+    rid, pid, _ = topo.addr(far)
+    mask = topo.mask(core, far)
+    g.wait_ge(T.sem.hc, got)
+    g.remote_dma(out_ap=T.kvc2[:].bitcast(dt.uint8), in_ap=T.kvc0[:].bitcast(dt.uint8), remote_sem=T.sem.arr2,
+                 local_sem=T.sem.sent, pid=pid, routing_id=rid, dma_engine_mask=mask)
+    g.wait_ge(T.sem.hs, got)
+    g.remote_dma(out_ap=T.kvs2[:], in_ap=T.kvs0[:], remote_sem=T.sem.arr2,
+                 local_sem=T.sem.sent, pid=pid, routing_id=rid, dma_engine_mask=mask)
+    g.wait_ge(T.sem.sent, 2 * engines(mask))
+
+
 def rank_program(g, core, T, topo):
     rank = T.rank_of(core)
     if rank is None:
+        for owner in T.cores:
+            if helper_of(owner, T, topo) == core:
+                forward(g, core, owner, T, topo)
         return
     n_ranks = len(T.cores)
     ALU, ACT = AluOpType, ActivationFunctionType
@@ -99,18 +129,22 @@ def rank_program(g, core, T, topo):
     op("dve", ["qin"], ["Q"], lambda: V.quantize_mx(T.qc[:], T.qs[:], T.qin[:]))
 
     deps("pool", ["kv0"], [])
-    for d in (2, 1):
-        dst = T.cores[(rank + d) % n_ranks]
-        rid, pid, _ = topo.addr(dst)
-        mask = topo.mask(core, dst)
-        eng = bin(mask).count("1")
-        g.remote_dma(out_ap=T["kvc%d" % d][:].bitcast(dt.uint8), in_ap=T.kvc0[:].bitcast(dt.uint8),
-                     remote_sem=T.sem["arr%d" % d], local_sem=T.sem.sent, pid=pid, routing_id=rid, dma_engine_mask=mask)
-        g.remote_dma(out_ap=T["kvs%d" % d][:], in_ap=T.kvs0[:],
-                     remote_sem=T.sem["arr%d" % d], local_sem=T.sem.sent, pid=pid, routing_id=rid, dma_engine_mask=mask)
-        count["sent"] = count.get("sent", 0) + 2 * eng
-        src = T.cores[(rank - d) % n_ranks]
-        count["arr%d" % d] = 2 * bin(topo.mask(src, core)).count("1")
+    near = T.cores[(rank + 1) % n_ranks]
+    hlp = helper_of(core, T, topo)
+    off = topo.mask(core, near)
+    on = topo.mask(core, hlp) & ~off
+    for buf, hsem in (("kvc", "hc"), ("kvs", "hs")):
+        for dst, mask, name, sem in ((hlp, on, buf + "0", hsem), (near, off, buf + "1", "arr1")):
+            rid, pid, _ = topo.addr(dst)
+            o_ap, i_ap = T[name][:], T[buf + "0"][:]
+            if buf == "kvc":
+                o_ap, i_ap = o_ap.bitcast(dt.uint8), i_ap.bitcast(dt.uint8)
+            g.remote_dma(out_ap=o_ap, in_ap=i_ap, remote_sem=T.sem[sem], local_sem=T.sem.sent,
+                         pid=pid, routing_id=rid, dma_engine_mask=mask)
+            count["sent"] = count.get("sent", 0) + engines(mask)
+    count["arr1"] = 2 * engines(topo.mask(T.cores[(rank - 1) % n_ranks], core))
+    count["arr2"] = 2 * engines(topo.mask(helper_of(T.cores[(rank - 2) % n_ranks], T, topo), core))
+    for d in (1, 2):
         writer["kv%d" % d] = ("arr%d" % d, count["arr%d" % d])
 
     def to_row(f, gt, fkey, gkey, width):
@@ -118,9 +152,8 @@ def rank_program(g, core, T, topo):
             op("dve", [fkey], [fkey], lambda: V.tensor_copy(f[0:32, 32 * a:width:128], f[32 * a:32 * a + 32, 0:width:128]))
         op("dve", [fkey], [gkey], lambda: V.transpose(gt[0:32, 0:width], f[0:32, 0:width]))
 
-    def scores(i, prev):
-        kc, ks, kv = T["kvc%d" % i], T["kvs%d" % i], "kv%d" % i
-        fc, gc, cbc, ssc = T["fc%d" % i], T["gc%d" % i], T["cbc%d" % i], T["ssc%d" % i]
+    def maxima(i, prev):
+        kc, ks, kv, fc = T["kvc%d" % i], T["kvs%d" % i], "kv%d" % i, T["fc%d" % i]
         for h in (0, 1):
             op("pe", [kv, "Q"], ["bank%d" % (2 + h)], lambda: P.matmul_mx(
                 bank(2 + h, 512), T.qc[:, 128 * h:128 * h + 128], T.qs[:, 128 * h:128 * h + 128],
@@ -135,6 +168,9 @@ def rank_program(g, core, T, topo):
             else:
                 op("dve", ["craw%d" % i, "fc%d" % prev], ["fc%d" % i], lambda: V.tensor_scalar(
                     col, raw, SCALE, T["fc%d" % prev][:, 128 * h:128 * h + 1], ALU.mult, ALU.max))
+
+    def scaled(i):
+        kc, ks, kv, ssc = T["kvc%d" % i], T["kvs%d" % i], "kv%d" % i, T["ssc%d" % i]
         for pair in (0, 2):
             for b in (pair, pair + 1):
                 op("pe", [kv, "Q"], ["bank%d" % (b % 2)], lambda: P.matmul_mx(
@@ -143,16 +179,18 @@ def rank_program(g, core, T, topo):
             for b in (pair, pair + 1):
                 op("act", [], ["bank%d" % (b % 2), "ssc%d.%d" % (i, b)], lambda: S.activation(
                     ssc[:, 256 * b:256 * b + 256], bank(b % 2, 256), ACT.Copy, scale=SCALE))
-        to_row(fc, gc, "fc%d" % i, "gc%d" % i, 256)
-        op("pool", ["gc%d" % i], ["cbc%d" % i], lambda: g.partition_broadcast(cbc[:], gc[0:1, :], 128))
-        dma("sync", "stored", T.c[i:i + 1, :], gc[0:1, :], ["gc%d" % i], [])
 
-    def probs(i):
-        cbc, ssc, pt = T["cbc%d" % i], T["ssc%d" % i], T["pt%d" % i]
-        for b in range(4):
-            x = ssc[:, 256 * b:256 * b + 256]
-            op("dve", ["cbc%d" % i], ["ssc%d.%d" % (i, b)], lambda: V.tensor_tensor(x, x, cbc[:], ALU.subtract))
-            op("act", ["ssc%d.%d" % (i, b)], ["pt%d.%d" % (i, b)], lambda: S.activation(pt[:, b:1024:4], x, ACT.Exp))
+    def spread_c(i):
+        to_row(T["fc%d" % i], T["gc%d" % i], "fc%d" % i, "gc%d" % i, 256)
+        op("pool", ["gc%d" % i], ["cbc%d" % i], lambda: g.partition_broadcast(T["cbc%d" % i][:], T["gc%d" % i][0:1, :], 128))
+
+    def shifted(i, b, ci):
+        x = T["ssc%d" % i][:, 256 * b:256 * b + 256]
+        op("dve", ["cbc%d" % ci], ["ssc%d.%d" % (i, b)], lambda: V.tensor_tensor(x, x, T["cbc%d" % ci][:], ALU.subtract))
+        op("act", ["ssc%d.%d" % (i, b)], ["pt%d.%d" % (i, b)], lambda: S.activation(T["pt%d" % i][:, b:1024:4], x, ACT.Exp))
+
+    def packed(i):
+        pt = T["pt%d" % i]
         for b in range(4):
             y = pt[:, b:1024:4]
             op("dve", [], ["pt%d.%d" % (i, b)], lambda: V.tensor_scalar(y, y, FLOOR, None, ALU.max))
@@ -160,68 +198,66 @@ def rank_program(g, core, T, topo):
         op("dve", tiles, ["P%d" % i], lambda: V.quantize_mx(T["pc%d" % i][:], T["pp%d" % i][:], pt[:]))
         dma("sync", "stored", T.p[i], pt[:], tiles, [])
 
-    def sums(i):
+    def products(i, j, start, stop):
         pc, pp = T["pc%d" % i], T["pp%d" % i]
         for h in (0, 1):
             op("pe", ["P%d" % i, "ONE"], ["bank%d" % (4 + h)], lambda: P.matmul_mx(
                 bank(4 + h, 128), pc[:, 128 * h:128 * h + 128], pp[:, 128 * h:128 * h + 128],
-                T.onec[:], T.ones[:], True, True))
-
-    def values(i, j):
+                T.onec[:], T.ones[:], start, stop))
         op("pe", ["P%d" % i, "kv%d" % i], ["bank%d" % j], lambda: P.matmul_mx(
-            bank(j, 256), T["kvc%d" % i][:, 512:640], T["kvs%d" % i][:, 512:640],
-            T["pc%d" % i][:], T["pp%d" % i][:], True, True))
+            bank(j, 256), T["kvc%d" % i][:, 512:640], T["kvs%d" % i][:, 512:640], pc[:], pp[:], start, stop))
 
-    def keep_sums(slot):
-        for h in (0, 1):
-            op("dve", [], ["bank%d" % (4 + h), "lcol"], lambda: V.tensor_copy(
-                T.lcol[:, 2 * slot + h:2 * slot + h + 1], bank(4 + h, 1)))
+    x, y, z = 0, 1, 2
 
-    x, y, z = 0, 2, 1
+    maxima(x, None)
+    scaled(x)
+    spread_c(x)
+    dma("sync", "stored", T.c[x:x + 1, :], T.gc0[0:1, :], ["gc0"], [])
+    for name in ("fc2", "fw", "fr"):
+        op("dve", [], [name], lambda: V.memset(T[name][0:32, 0:256], 0.0))
+    op("dve", [], ["onef"], lambda: V.memset(T.onef[0:2, :], 1.0))
+    dma("sync", "stored", T.w[y:z + 1, :], T.onef[0:2, :], ["onef"], [])
+    for b in range(4):
+        shifted(x, b, x)
+    packed(x)
+    products(x, 6, True, True)
+    for h in (0, 1):
+        op("dve", [], ["bank%d" % (4 + h), "lcol"], lambda: V.tensor_copy(T.lcol[:, h:h + 1], bank(4 + h, 1)))
 
-    scores(x, None)
-    for name in ("fc1", "fc2", "fw", "fr"):
-        op("dve", [], [name], lambda: V.memset(T[name][0:32, :], 0.0))
-    op("dve", [], ["onef"], lambda: V.memset(T.onef[0:1, :], 1.0))
-    probs(x)
-    sums(x)
-    values(x, 6)
-    keep_sums(0)
-
-    scores(y, x)
-    probs(y)
-    sums(y)
-    values(y, 7)
-    keep_sums(1)
-
-    scores(z, y)
-    for slot, i in ((0, x), (1, y)):
-        op("dve", ["fc%d" % i, "fc%d" % z], ["dcol"], lambda: V.tensor_tensor(
-            T.dcol[:, 2 * slot:2 * slot + 2], T["fc%d" % i][:, 0:256:128], T["fc%d" % z][:, 0:256:128], ALU.subtract))
-    op("act", ["dcol"], ["fw"], lambda: S.activation(T.fw[:, 0:512:128], T.dcol[:, 0:4], ACT.Exp))
-    op("dve", ["fw", "lcol"], ["t4"], lambda: V.tensor_tensor(T.t4[:], T.lcol[:], T.fw[:, 0:512:128], ALU.mult))
-    to_row(T.fw, T.gw, "fw", "gw", 512)
-    op("pool", ["gw"], ["wbc"], lambda: g.partition_broadcast(T.wbc[:], T.gw[0:1, :], 128))
-    op("dve", ["t4"], ["t01"], lambda: V.tensor_tensor(T.t01[:], T.t4[:, 0:2], T.t4[:, 2:4], ALU.add))
+    maxima(y, x)
+    maxima(z, y)
+    scaled(y)
+    scaled(z)
+    spread_c(z)
+    dma("sync", "stored", T.c[y:z + 1, :], T.cbc2[0:2, :], ["cbc2"], [])
+    op("dve", ["fc0", "fc2"], ["dcol"], lambda: V.tensor_tensor(
+        T.dcol[:, 0:2], T.fc0[:, 0:256:128], T.fc2[:, 0:256:128], ALU.subtract))
+    op("act", ["dcol"], ["fw"], lambda: S.activation(T.fw[:, 0:256:128], T.dcol[:, 0:2], ACT.Exp))
+    for b in range(4):
+        shifted(y, b, z)
+    op("dve", ["fw", "lcol"], ["t01"], lambda: V.tensor_tensor(T.t01[:], T.lcol[:, 0:2], T.fw[:, 0:256:128], ALU.mult))
+    to_row(T.fw, T.gw, "fw", "gw", 256)
+    op("pool", ["gw"], ["wbc"], lambda: g.partition_broadcast(T.wbc[:, 0:256], T.gw[0:1, 0:256], 128))
     dma("sync", "stored", T.w[x:x + 1, :], T.gw[0:1, 0:256], ["gw"], [])
-    dma("sync", "stored", T.w[y:y + 1, :], T.gw[0:1, 256:512], ["gw"], [])
-    dma("sync", "stored", T.w[z:z + 1, :], T.onef[0:1, :], ["onef"], [])
-    probs(z)
-    sums(z)
-    values(z, 0)
-
+    shifted(z, 0, z)
+    packed(y)
+    products(y, 7, True, False)
+    for b in (1, 2, 3):
+        shifted(z, b, z)
     op("dve", ["wbc"], ["bank6", "n1"], lambda: V.tensor_tensor(T.n1[:], bank(6, 256), T.wbc[:, 0:256], ALU.mult))
+    packed(z)
+    products(z, 7, False, True)
+
     for h in (0, 1):
         op("dve", ["t01"], ["bank%d" % (4 + h), "den"], lambda: V.tensor_tensor(
             T.den[:, h:h + 1], bank(4 + h, 1), T.t01[:, h:h + 1], ALU.add))
     op("dve", ["den"], ["fr"], lambda: V.reciprocal(T.fr[:, 0:256:128], T.den[:]))
     to_row(T.fr, T.gr, "fr", "gr", 256)
     op("pool", ["gr"], ["rbc"], lambda: g.partition_broadcast(T.rbc[:], T.gr[0:1, :], 128))
-    op("dve", ["wbc"], ["bank7", "n2"], lambda: V.tensor_tensor(T.n2[:], bank(7, 256), T.wbc[:, 256:512], ALU.mult))
-    op("dve", ["n2"], ["n1"], lambda: V.tensor_tensor(T.n1[:], T.n1[:], T.n2[:], ALU.add))
-    op("dve", [], ["bank0", "n1"], lambda: V.tensor_tensor(T.n1[:], bank(0, 256), T.n1[:], ALU.add))
+    op("dve", [], ["bank7", "n1"], lambda: V.tensor_tensor(T.n1[:], bank(7, 256), T.n1[:], ALU.add))
     op("dve", ["n1", "rbc"], ["ob"], lambda: V.tensor_tensor(T.ob[:], T.n1[:], T.rbc[:], ALU.mult))
     dma("sync", "stored", T.o[:], T.ob[:], ["ob"], [])
 
     for s in SEMAPHORES:
-        need("pool", (s, count[s]))
+        if s in count:
+            need("pool", (s, count[s]))

import math
from concourse.mybir import dt, AluOpType, AxisListType, ActivationFunctionType

F32, BF, CODE, U8 = "float32", "bfloat16", "float8_e4m3fn_x4", "uint8"
SCRATCH = {
    "kin": ("sbuf", [128, 2048], BF), "vin": ("sbuf", [128, 512], BF), "qin": ("sbuf", [128, 1024], BF),
    "one": ("sbuf", [128, 512], BF),
    "qc": ("sbuf", [128, 256], CODE), "qs": ("sbuf", [128, 256], U8),
    "onec": ("sbuf", [128, 128], CODE), "ones": ("sbuf", [128, 128], U8),
    "fw": ("sbuf", [128, 256], F32), "gw": ("sbuf", [128, 256], F32), "wbc": ("sbuf", [128, 256], F32),
    "fr": ("sbuf", [128, 256], F32), "gr": ("sbuf", [128, 256], F32), "rbc": ("sbuf", [128, 256], F32),
    "craw": ("sbuf", [128, 8], F32), "dcol": ("sbuf", [128, 2], F32), "lcol": ("sbuf", [128, 2], F32),
    "t01": ("sbuf", [128, 2], F32), "den": ("sbuf", [128, 2], F32),
    "onef": ("sbuf", [128, 256], F32), "n1": ("sbuf", [128, 256], F32), "ob": ("sbuf", [128, 256], F32),
    "ps": ("psum", [128, 4096], F32),
}
for _i in range(3):
    SCRATCH["kvc%d" % _i] = ("sbuf", [128, 640], CODE)
    SCRATCH["kvs%d" % _i] = ("sbuf", [128, 640], U8)
    SCRATCH["ssc%d" % _i] = ("sbuf", [128, 1024], F32)
    SCRATCH["pt%d" % _i] = ("sbuf", [128, 1024], BF)
    SCRATCH["pc%d" % _i] = ("sbuf", [128, 256], CODE)
    SCRATCH["pp%d" % _i] = ("sbuf", [128, 256], U8)
    SCRATCH["fc%d" % _i] = ("sbuf", [128, 256], F32)
    SCRATCH["gc%d" % _i] = ("sbuf", [128, 256], F32)
    SCRATCH["cbc%d" % _i] = ("sbuf", [128, 256], F32)

SEMAPHORES = ["dve", "act", "pe", "pool", "sent", "arr1", "arr2", "ld_k0", "ld_k1", "ld_v", "ld_q", "stored", "hc", "hs"]

SCALE = 0.0125
FLOOR = math.exp(-20.0)


def engines(mask):
    return bin(mask).count("1")


def helper_of(c, T, topo):
    far = T.cores[(T.rank_of(c) + 2) % len(T.cores)]
    for h in range(topo.CHIPS * topo.CORES_PER_CHIP):
        if h != c and topo.chip(h) == topo.chip(c) and topo.die(h) != topo.die(c) \
                and T.rank_of(h) is None and topo.may_write(h, far):
            return h
    return None


def forward(g, core, owner, T, topo):
    far = T.cores[(T.rank_of(owner) + 2) % len(T.cores)]
    near = T.cores[(T.rank_of(owner) + 1) % len(T.cores)]
    got = engines(topo.mask(owner, core) & ~topo.mask(owner, near))
    rid, pid, _ = topo.addr(far)
    mask = topo.mask(core, far)
    g.wait_ge(T.sem.hc, got)
    g.remote_dma(out_ap=T.kvc2[:].bitcast(dt.uint8), in_ap=T.kvc0[:].bitcast(dt.uint8), remote_sem=T.sem.arr2,
                 local_sem=T.sem.sent, pid=pid, routing_id=rid, dma_engine_mask=mask)
    g.wait_ge(T.sem.hs, got)
    g.remote_dma(out_ap=T.kvs2[:], in_ap=T.kvs0[:], remote_sem=T.sem.arr2,
                 local_sem=T.sem.sent, pid=pid, routing_id=rid, dma_engine_mask=mask)
    g.wait_ge(T.sem.sent, 2 * engines(mask))


def rank_program(g, core, T, topo):
    rank = T.rank_of(core)
    if rank is None:
        for owner in T.cores:
            if helper_of(owner, T, topo) == core:
                forward(g, core, owner, T, topo)
        return
    n_ranks = len(T.cores)
    ALU, ACT = AluOpType, ActivationFunctionType
    queue = {"dve": g.vector, "act": g.scalar, "pe": g.tensor, "pool": g, "sync": g.sync}
    count = {}
    seen = {}
    writer = {}
    readers = {}

    def need(q, ticket):
        if ticket is None:
            return
        s, n = ticket
        if seen.get((q, s), 0) < n:
            queue[q].wait_ge(T.sem[s], n)
            seen[(q, s)] = n

    def deps(q, reads, writes):
        for k in reads:
            need(q, writer.get(k))
        for k in writes:
            need(q, writer.get(k))
            for t in readers.get(k, []):
                need(q, t)

    def note(ticket, reads, writes):
        for k in reads:
            readers.setdefault(k, []).append(ticket)
        for k in writes:
            writer[k] = ticket
            readers[k] = []

    def op(q, reads, writes, make):
        deps(q, reads, writes)
        count[q] = count.get(q, 0) + 1
        make().then_inc(T.sem[q], 1)
        note((q, count[q]), reads, writes)

    def dma(q, sem, out, in_, reads, writes):
        deps(q, reads, writes)
        count[sem] = count.get(sem, 0) + 16
        queue[q].dma_start(out, in_).then_inc(T.sem[sem], 16)
        note((sem, count[sem]), reads, writes)

    def bank(j, n):
        return T.ps[:, 512 * j:512 * j + n]

    V, S, P = g.vector, g.scalar, g.tensor

    dma("sync", "ld_k0", T.kin[:, 0:1024], T.k[:, 0:1024], [], ["kin0"])
    dma("act", "ld_k1", T.kin[:, 1024:2048], T.k[:, 1024:2048], [], ["kin1"])
    dma("sync", "ld_v", T.vin[:], T.v[:], [], ["vin"])
    dma("act", "ld_q", T.qin[:], T.q[:], [], ["qin"])

    op("dve", [], ["one"], lambda: V.memset(T.one[:], 1.0))
    op("dve", ["one"], ["ONE"], lambda: V.quantize_mx(T.onec[:], T.ones[:], T.one[:]))
    op("dve", [], ["fc0"], lambda: V.memset(T.fc0[0:32, :], 0.0))

    op("dve", ["kin0"], ["kv0"], lambda: V.quantize_mx(T.kvc0[:, 0:256], T.kvs0[:, 0:256], T.kin[:, 0:1024]))
    op("dve", ["kin1"], ["kv0"], lambda: V.quantize_mx(T.kvc0[:, 256:512], T.kvs0[:, 256:512], T.kin[:, 1024:2048]))
    op("dve", ["vin"], ["kv0"], lambda: V.quantize_mx(T.kvc0[:, 512:640], T.kvs0[:, 512:640], T.vin[:]))
    op("dve", ["qin"], ["Q"], lambda: V.quantize_mx(T.qc[:], T.qs[:], T.qin[:]))

    deps("pool", ["kv0"], [])
    near = T.cores[(rank + 1) % n_ranks]
    hlp = helper_of(core, T, topo)
    off = topo.mask(core, near)
    on = topo.mask(core, hlp) & ~off
    for buf, hsem in (("kvc", "hc"), ("kvs", "hs")):
        for dst, mask, name, sem in ((hlp, on, buf + "0", hsem), (near, off, buf + "1", "arr1")):
            rid, pid, _ = topo.addr(dst)
            o_ap, i_ap = T[name][:], T[buf + "0"][:]
            if buf == "kvc":
                o_ap, i_ap = o_ap.bitcast(dt.uint8), i_ap.bitcast(dt.uint8)
            g.remote_dma(out_ap=o_ap, in_ap=i_ap, remote_sem=T.sem[sem], local_sem=T.sem.sent,
                         pid=pid, routing_id=rid, dma_engine_mask=mask)
            count["sent"] = count.get("sent", 0) + engines(mask)
    count["arr1"] = 2 * engines(topo.mask(T.cores[(rank - 1) % n_ranks], core))
    count["arr2"] = 2 * engines(topo.mask(helper_of(T.cores[(rank - 2) % n_ranks], T, topo), core))
    for d in (1, 2):
        writer["kv%d" % d] = ("arr%d" % d, count["arr%d" % d])

    def to_row(f, gt, fkey, gkey, width):
        for a in (1, 2, 3):
            op("dve", [fkey], [fkey], lambda: V.tensor_copy(f[0:32, 32 * a:width:128], f[32 * a:32 * a + 32, 0:width:128]))
        op("dve", [fkey], [gkey], lambda: V.transpose(gt[0:32, 0:width], f[0:32, 0:width]))

    def maxima(i, prev):
        kc, ks, kv, fc = T["kvc%d" % i], T["kvs%d" % i], "kv%d" % i, T["fc%d" % i]
        for h in (0, 1):
            op("pe", [kv, "Q"], ["bank%d" % (2 + h)], lambda: P.matmul_mx(
                bank(2 + h, 512), T.qc[:, 128 * h:128 * h + 128], T.qs[:, 128 * h:128 * h + 128],
                kc[:, 0:512], ks[:, 0:512], True, True))
        for h in (0, 1):
            raw = T.craw[:, 2 * i + h:2 * i + h + 1]
            op("dve", [], ["bank%d" % (2 + h), "craw%d" % i], lambda: V.tensor_reduce(
                raw, bank(2 + h, 512), AxisListType.X, ALU.max))
            col = fc[:, 128 * h:128 * h + 1]
            if prev is None:
                op("dve", ["craw%d" % i], ["fc%d" % i], lambda: V.tensor_scalar(col, raw, SCALE, None, ALU.mult))
            else:
                op("dve", ["craw%d" % i, "fc%d" % prev], ["fc%d" % i], lambda: V.tensor_scalar(
                    col, raw, SCALE, T["fc%d" % prev][:, 128 * h:128 * h + 1], ALU.mult, ALU.max))

    def scaled(i):
        kc, ks, kv, ssc = T["kvc%d" % i], T["kvs%d" % i], "kv%d" % i, T["ssc%d" % i]
        for pair in (0, 2):
            for b in (pair, pair + 1):
                op("pe", [kv, "Q"], ["bank%d" % (b % 2)], lambda: P.matmul_mx(
                    bank(b % 2, 256), kc[:, 128 * b:128 * b + 128], ks[:, 128 * b:128 * b + 128],
                    T.qc[:], T.qs[:], True, True))
            for b in (pair, pair + 1):
                op("act", [], ["bank%d" % (b % 2), "ssc%d.%d" % (i, b)], lambda: S.activation(
                    ssc[:, 256 * b:256 * b + 256], bank(b % 2, 256), ACT.Copy, scale=SCALE))

    def spread_c(i):
        to_row(T["fc%d" % i], T["gc%d" % i], "fc%d" % i, "gc%d" % i, 256)
        op("pool", ["gc%d" % i], ["cbc%d" % i], lambda: g.partition_broadcast(T["cbc%d" % i][:], T["gc%d" % i][0:1, :], 128))

    def shifted(i, b, ci):
        x = T["ssc%d" % i][:, 256 * b:256 * b + 256]
        op("dve", ["cbc%d" % ci], ["ssc%d.%d" % (i, b)], lambda: V.tensor_tensor(x, x, T["cbc%d" % ci][:], ALU.subtract))
        op("act", ["ssc%d.%d" % (i, b)], ["pt%d.%d" % (i, b)], lambda: S.activation(T["pt%d" % i][:, b:1024:4], x, ACT.Exp))

    def packed(i):
        pt = T["pt%d" % i]
        for b in range(4):
            y = pt[:, b:1024:4]
            op("dve", [], ["pt%d.%d" % (i, b)], lambda: V.tensor_scalar(y, y, FLOOR, None, ALU.max))
        tiles = ["pt%d.%d" % (i, b) for b in range(4)]
        op("dve", tiles, ["P%d" % i], lambda: V.quantize_mx(T["pc%d" % i][:], T["pp%d" % i][:], pt[:]))
        dma("sync", "stored", T.p[i], pt[:], tiles, [])

    def products(i, j, start, stop):
        pc, pp = T["pc%d" % i], T["pp%d" % i]
        for h in (0, 1):
            op("pe", ["P%d" % i, "ONE"], ["bank%d" % (4 + h)], lambda: P.matmul_mx(
                bank(4 + h, 128), pc[:, 128 * h:128 * h + 128], pp[:, 128 * h:128 * h + 128],
                T.onec[:], T.ones[:], start, stop))
        op("pe", ["P%d" % i, "kv%d" % i], ["bank%d" % j], lambda: P.matmul_mx(
            bank(j, 256), T["kvc%d" % i][:, 512:640], T["kvs%d" % i][:, 512:640], pc[:], pp[:], start, stop))

    x, y, z = 0, 1, 2

    maxima(x, None)
    scaled(x)
    spread_c(x)
    dma("sync", "stored", T.c[x:x + 1, :], T.gc0[0:1, :], ["gc0"], [])
    for name in ("fc2", "fw", "fr"):
        op("dve", [], [name], lambda: V.memset(T[name][0:32, 0:256], 0.0))
    op("dve", [], ["onef"], lambda: V.memset(T.onef[0:2, :], 1.0))
    dma("sync", "stored", T.w[y:z + 1, :], T.onef[0:2, :], ["onef"], [])
    for b in range(4):
        shifted(x, b, x)
    packed(x)
    products(x, 6, True, True)
    for h in (0, 1):
        op("dve", [], ["bank%d" % (4 + h), "lcol"], lambda: V.tensor_copy(T.lcol[:, h:h + 1], bank(4 + h, 1)))

    maxima(y, x)
    maxima(z, y)
    scaled(y)
    scaled(z)
    spread_c(z)
    dma("sync", "stored", T.c[y:z + 1, :], T.cbc2[0:2, :], ["cbc2"], [])
    op("dve", ["fc0", "fc2"], ["dcol"], lambda: V.tensor_tensor(
        T.dcol[:, 0:2], T.fc0[:, 0:256:128], T.fc2[:, 0:256:128], ALU.subtract))
    op("act", ["dcol"], ["fw"], lambda: S.activation(T.fw[:, 0:256:128], T.dcol[:, 0:2], ACT.Exp))
    for b in range(4):
        shifted(y, b, z)
    op("dve", ["fw", "lcol"], ["t01"], lambda: V.tensor_tensor(T.t01[:], T.lcol[:, 0:2], T.fw[:, 0:256:128], ALU.mult))
    to_row(T.fw, T.gw, "fw", "gw", 256)
    op("pool", ["gw"], ["wbc"], lambda: g.partition_broadcast(T.wbc[:, 0:256], T.gw[0:1, 0:256], 128))
    dma("sync", "stored", T.w[x:x + 1, :], T.gw[0:1, 0:256], ["gw"], [])
    shifted(z, 0, z)
    packed(y)
    products(y, 7, True, False)
    for b in (1, 2, 3):
        shifted(z, b, z)
    op("dve", ["wbc"], ["bank6", "n1"], lambda: V.tensor_tensor(T.n1[:], bank(6, 256), T.wbc[:, 0:256], ALU.mult))
    packed(z)
    products(z, 7, False, True)

    for h in (0, 1):
        op("dve", ["t01"], ["bank%d" % (4 + h), "den"], lambda: V.tensor_tensor(
            T.den[:, h:h + 1], bank(4 + h, 1), T.t01[:, h:h + 1], ALU.add))
    op("dve", ["den"], ["fr"], lambda: V.reciprocal(T.fr[:, 0:256:128], T.den[:]))
    to_row(T.fr, T.gr, "fr", "gr", 256)
    op("pool", ["gr"], ["rbc"], lambda: g.partition_broadcast(T.rbc[:], T.gr[0:1, :], 128))
    op("dve", [], ["bank7", "n1"], lambda: V.tensor_tensor(T.n1[:], bank(7, 256), T.n1[:], ALU.add))
    op("dve", ["n1", "rbc"], ["ob"], lambda: V.tensor_tensor(T.ob[:], T.n1[:], T.rbc[:], ALU.mult))
    dma("sync", "stored", T.o[:], T.ob[:], ["ob"], [])

    for s in SEMAPHORES:
        if s in count:
            need("pool", (s, count[s]))
